import numpy as np
import ml_dtypes


def mxq(x, axis, fmt="e4m3"):
    dtype, down = {"e4m3": (ml_dtypes.float8_e4m3fn, 7), "e5m2": (ml_dtypes.float8_e5m2, 14)}[fmt]
    v = np.moveaxis(np.asarray(x, np.float32).astype(ml_dtypes.bfloat16).astype(np.float64), axis, -1)
    blocks = v.reshape(v.shape[:-1] + (-1, 32))
    amax = np.abs(blocks).max(-1, keepdims=True)
    byte = np.maximum(np.where(amax > 0, np.frexp(amax)[1] - 1 + 127, 0) - down, 1)
    scale = np.exp2(byte - 127.0)
    codes = (blocks / scale).astype(np.float32).astype(dtype).astype(np.float64)
    return np.moveaxis((codes * scale).reshape(v.shape), -1, axis)


WIDE = False


def mx_kscale(k):
    if not WIDE:
        return np.ones(k)
    levels = np.array([10, -10, 5, -5, 0])
    if k % 512:
        return np.exp2(np.random.permutation(np.resize(levels, k // 32))).repeat(32)
    a = np.empty((k // 512, 16))
    for p in range(k // 512):
        a[p, :8] = np.random.permutation(np.resize(levels, 8))
        for g in range(8):
            far = levels[np.abs(levels - a[p, g]) >= 10]
            a[p, g + 8] = far[np.random.randint(len(far))]
    return np.exp2(a.ravel()).repeat(32)


def f64(x):
    return np.asarray(x).astype(np.float64)


def striped(idx):
    return np.tile(np.asarray(idx).reshape(-1, 16).T, (8, 1)).astype(np.uint16)


def unstriped(offs):
    return offs[:16].T.reshape(-1).astype(np.int64)


E2M1 = np.array([0.0, 0.5, 1.0, 1.5, 2.0, 3.0, 4.0, 6.0, -0.0, -0.5, -1.0, -1.5, -2.0, -3.0, -4.0, -6.0])


def pack_weight(w, fmt):
    k, n = w.shape
    w = f64(np.asarray(w, np.float32).astype(ml_dtypes.bfloat16)).reshape(k // 32, 32, n)
    amax = np.abs(w).max(1)
    if fmt == "e4m3":
        byte = np.frexp(amax)[1] - 1 + 127 - 7
    else:
        mant, ex = np.frexp(amax / 6.0)
        byte = np.where(mant > 0.5, ex, ex - 1) + 127
    byte = np.clip(np.where(amax > 0, byte, 1), 1, 254)
    scaled = (w * np.exp2(127.0 - byte)[:, None, :]).reshape(k, n).astype(np.float32)
    by_word = np.ascontiguousarray(scaled.reshape(k // 512, 128, 4, n).transpose(0, 1, 3, 2))
    if fmt == "e4m3":
        words = by_word.astype(ml_dtypes.float8_e4m3fn).view(np.uint8)
    else:
        c = by_word.astype(ml_dtypes.float4_e2m1fn).view(np.uint8) & 0xF
        words = (c[..., 0::2] | (c[..., 1::2] << 4)).reshape(k // 512, 128, 2 * n)
    return np.ascontiguousarray(words), np.ascontiguousarray(byte.astype(np.uint8).reshape(k // 512, 16, n))


def unpack_weight(words, scales, fmt):
    g, _, n = scales.shape
    words = np.ascontiguousarray(words).reshape(g, 128, n, -1)
    if fmt == "e4m3":
        vals = words.view(ml_dtypes.float8_e4m3fn).astype(np.float64)
    else:
        nib = np.empty((g, 128, n, 4), np.uint8)
        nib[..., 0::2] = words & 0xF
        nib[..., 1::2] = words >> 4
        vals = E2M1[nib]
    vals = vals * np.repeat(np.exp2(scales.astype(np.float64) - 127.0), 8, axis=1)[..., None]
    return vals.transpose(0, 1, 3, 2).reshape(g * 512, n)


def sigmoid(v):
    return 1.0 / (1.0 + np.exp(-v))


D, T, I, Q = 512, 1024, 512, 128


def setup_inputs():
    n = np.random.standard_normal
    idx = np.random.permutation(T)[:I]
    idx2 = np.random.permutation(T)[:I]
    fd = mx_kscale(D)
    fi = mx_kscale(I)
    candp = pack_weight(n((D, T)) / fd[:, None], "e4m3")
    return {
        "query": (n((D, Q)) * 1.0 / np.sqrt(D) * fd[:, None]).astype(np.float32),
        "cand_words": candp[0],
        "cand_scales": candp[1],
        "crow": (n((D, T))).astype(np.float32),
        "psz": (np.random.uniform(0.5, 2.0, (1, I)) * fi).astype(np.float32),
        "ds1": (np.random.uniform(0.3, 1.0, (I, 1)) / fi[:, None]).astype(np.float32),
        "res": (n((Q, D)) * 4.0).astype(np.float32),
        "offs": striped(idx),
        "offs2": striped(idx2),
    }


def reference(query, cand_words, cand_scales, crow, psz, ds1, res, offs, offs2):
    idx = unstriped(offs)
    idx2 = unstriped(offs2)
    candu = unpack_weight(cand_words, cand_scales, "e4m3")
    queryq = mxq(f64(query), 0, "e4m3")
    candidxg = candu[:, idx]
    a = queryq.T @ candidxg
    candidx2g = candu[:, idx2]
    b = queryq.T @ candidx2g
    s = sigmoid(b - a) * f64(psz)
    st = s.T
    ka = f64(crow)[:, idx].T
    kb = f64(crow)[:, idx2].T
    kd = (kb - ka) * f64(ds1)
    stq = mxq(st, 0, "e4m3")
    kdq = mxq(kd, 0, "e4m3")
    gq = stq.T @ kdq
    y = gq + f64(res)
    return y

@@ -1,0 +1,161 @@
+from contextlib import ExitStack
+
+import concourse.mybir as mybir
+from concourse.masks import make_identity
+
+D, T, I, Q = 512, 1024, 512, 128
+P = 128
+PACK = 4
+TILES = D // P
+FLOPS = 2 * Q * I * D * 3
+
+F32 = mybir.dt.float32
+BF16 = mybir.dt.bfloat16
+I32 = mybir.dt.int32
+U32 = mybir.dt.uint32
+U16 = mybir.dt.uint16
+U8 = mybir.dt.uint8
+FP8X4 = mybir.dt.float8_e4m3fn_x4
+ACT = mybir.ActivationFunctionType
+ALU = mybir.AluOpType
+
+
+def tile_attend_gpairrank_kernel(tc, query, cand_words, cand_scales, crow, psz, ds1, res, offs, offs2, out):
+    nc = tc.nc
+    with ExitStack() as ctx:
+        sb = ctx.enter_context(tc.tile_pool(name="sb", bufs=1))
+        ps = ctx.enter_context(tc.psum_pool(name="ps", bufs=1))
+
+        list_a = sb.tile([P, I // 16], U16, name="list_a")
+        list_b = sb.tile([P, I // 16], U16, name="list_b")
+        scale_win = sb.tile([P, T], U8, name="scale_win")
+        word_win = sb.tile([P, T], I32, name="word_win")
+        q_raw = sb.tile([P, PACK, Q], F32, name="q_raw")
+        row_win = [sb.tile([P, 2 * T], F32, name="row_win%d" % j) for j in range(TILES)]
+        psz_t = sb.tile([P, PACK], F32, name="psz_t")
+        ds1_t = sb.tile([P, PACK], F32, name="ds1_t")
+        res_t = sb.tile([P, D], F32, name="res_t")
+        ident = sb.tile([P, P], F32, name="ident")
+        warm = sb.tile([P, 8], F32, name="warm")
+        warm_out = sb.tile([P, 8], F32, name="warm_out")
+
+        nc.gpsimd.memset(scale_win[:].bitcast(I32), 0)
+        nc.sync.dma_start(list_a[:], offs)
+        for quad in range(4):
+            queue = nc.sync if quad < 2 else nc.scalar
+            queue.dma_start(
+                out=scale_win[32 * quad : 32 * quad + 4, :].bitcast(I32),
+                in_=cand_scales[0, 4 * quad : 4 * quad + 4, :].bitcast(I32),
+            )
+        nc.sync.dma_start(list_b[:], offs2)
+        nc.sync.dma_start(out=psz_t[:], in_=psz.rearrange("o (p t) -> (o p) t", t=PACK))
+        nc.vector.memset(warm[:], 0.0)
+        nc.scalar.activation(warm_out[:], warm[:], ACT.Sigmoid)
+        nc.sync.dma_start(out=word_win[:], in_=cand_words[0].rearrange("p n t -> p (n t)").bitcast(I32))
+        nc.sync.dma_start(out=q_raw[:], in_=query.rearrange("(p t) q -> p t q", t=PACK))
+        nc.sync.dma_start(out=row_win[0][:, 0:T], in_=crow[0:P, :])
+        nc.sync.dma_start(out=ds1_t[:], in_=ds1.rearrange("(p t) o -> p (t o)", t=PACK))
+        for j in range(1, TILES):
+            nc.sync.dma_start(out=row_win[j][:, 0:T], in_=crow[j * P : (j + 1) * P, :])
+        nc.sync.dma_start(out=res_t[:], in_=res)
+        make_identity(nc, ident[:])
+
+        def scale_and_group(bank, factor, grouped):
+            planes = sb.tile([P, PACK, P], BF16, name="planes")
+            for t in range(PACK):
+                nc.scalar.activation(planes[:, t, :], bank[:, t, :], ACT.Copy, scale=factor[:, t : t + 1])
+            nc.scalar.copy(
+                out=grouped.rearrange("p (c i) t -> p c t i", i=4),
+                in_=planes[:].rearrange("p t (c i) -> p c t i", i=4),
+            )
+
+        def turned_difference(j, sb_tag, ps_tag):
+            pair = sb.tile([P, 2, I], F32, name="pair%d" % j, tag=sb_tag, align_bytes=64)
+            nc.vector.tensor_scalar(pair[:, 0, :], row_win[j][:].indirect(list_a[:]), -1.0, 0.0, ALU.mult, ALU.add)
+            nc.vector.tensor_copy(
+                pair[:, 1, :].bitcast(U32).rearrange("p (t s) -> p s t", t=PACK),
+                row_win[j][:, 0:T].bitcast(U32).indirect(list_b[:]),
+            )
+            bank = ps.tile([P, PACK, P], F32, name="kd_bank%d" % j, tag=ps_tag)
+            for t in range(PACK):
+                nc.tensor.matmul(bank[:, t, :], pair[:, 0, t:I:PACK], ident[:], start=(t == 0), stop=False, is_transpose=True)
+            for t in range(PACK):
+                nc.tensor.matmul(
+                    bank[:, t, :], pair[:, 1, t * P : (t + 1) * P], ident[:], start=False, stop=(t == PACK - 1), is_transpose=True
+                )
+            return bank
+
+        def quantise(grouped, width, name):
+            codes = sb.tile([P, width], U32, name=name + "_codes", align_bytes=64)
+            scales = sb.tile([P, width], U8, name=name + "_scales", align_bytes=64)
+            nc.vector.quantize_mx(out=codes[:].bitcast(FP8X4), scales=scales[:], in_=grouped)
+            return codes, scales
+
+        def product(acc, lhs, lhs_cols, rhs, rhs_cols, start, stop):
+            nc.tensor.matmul_mx(
+                out=acc,
+                lhsT=lhs[0][:, lhs_cols].bitcast(FP8X4),
+                lhsT_scale=lhs[1][:, lhs_cols],
+                rhs=rhs[0][:, rhs_cols].bitcast(FP8X4),
+                rhs_scale=rhs[1][:, rhs_cols],
+                start=start,
+                stop=stop,
+            )
+
+        def finish(acc, first, width, name):
+            cols = slice(first, first + width)
+            y = sb.tile([P, width], F32, name=name)
+            nc.vector.tensor_tensor(y[:], acc, res_t[:, cols], ALU.add)
+            nc.sync.dma_start(out=out[:, cols], in_=y[:])
+
+        scale_a = sb.tile([P, I], U8, name="scale_a", align_bytes=64)
+        scale_b = sb.tile([P, I], U8, name="scale_b", align_bytes=64)
+        nc.vector.tensor_copy(scale_a[:], scale_win[:].indirect(list_a[:]))
+        nc.vector.tensor_copy(scale_b[:], scale_win[:].indirect(list_b[:]))
+        word_a = sb.tile([P, I], U32, name="word_a", align_bytes=64)
+        word_b = sb.tile([P, I], U32, name="word_b", align_bytes=64)
+        nc.vector.tensor_copy(word_a[:], word_win[:].bitcast(U32).indirect(list_a[:]))
+        nc.vector.tensor_copy(word_b[:], word_win[:].bitcast(U32).indirect(list_b[:]))
+
+        q_grp = sb.tile([P, 2, Q, PACK], BF16, name="q_grp", tag="q_then_pair0", align_bytes=64)
+        for u, sign in enumerate((-1.0, 1.0)):
+            nc.scalar.activation(q_grp[:, u, :, :], q_raw[:].rearrange("p t q -> p q t"), ACT.Copy, scale=sign)
+        q_mx = quantise(q_grp[:].rearrange("p u q t -> p (u q t)"), 2 * Q, "q")
+
+        z = ps.tile([P, I], F32, name="z")
+        product(z[:], q_mx, slice(0, Q), (word_a, scale_a), slice(0, I), True, False)
+        product(z[:], q_mx, slice(Q, 2 * Q), (word_b, scale_b), slice(0, I), False, True)
+
+        grouped = sb.tile([P, TILES, P, PACK], BF16, name="grouped", tag="grouped", align_bytes=64)
+
+        sig = sb.tile([P, PACK, P], F32, name="sig")
+        nc.scalar.activation(sig[:], z[:].rearrange("q (s t) -> q t s", t=PACK), ACT.Sigmoid)
+        bank0 = turned_difference(0, "q_then_pair0", "bank_even")
+        s_bank = ps.tile([P, PACK, Q], F32, name="s_bank", tag="bank_odd")
+        for t in range(PACK):
+            nc.tensor.transpose(s_bank[:, t, :], sig[:, t, :], ident[:])
+        scale_and_group(s_bank, psz_t, grouped[:, 0, :, :])
+        bank1 = turned_difference(1, "pair1", "bank_odd")
+        scale_and_group(bank0, ds1_t, grouped[:, 1, :, :])
+        bank2 = turned_difference(2, "pair2", "bank_even")
+        scale_and_group(bank1, ds1_t, grouped[:, 2, :, :])
+        bank3 = turned_difference(3, "pair3", "bank_odd")
+        scale_and_group(bank2, ds1_t, grouped[:, 3, :, :])
+
+        main_mx = quantise(grouped[:].rearrange("p j d t -> p (j d t)"), TILES * P, "main")
+        acc = ps.tile([P, 3 * P], F32, name="acc")
+        product(acc[:, 0 : 2 * P], main_mx, slice(0, Q), main_mx, slice(P, 3 * P), True, True)
+        product(acc[:, 2 * P : 3 * P], main_mx, slice(0, Q), main_mx, slice(3 * P, 4 * P), True, True)
+
+        kd3 = sb.tile([P, P, PACK], BF16, name="kd3", tag="grouped", align_bytes=64)
+        nc.vector.tensor_tensor(
+            kd3[:],
+            bank3[:].rearrange("p t d -> p d t"),
+            ds1_t[:].unsqueeze(1).to_broadcast([P, P, PACK]),
+            ALU.mult,
+        )
+        kd3_mx = quantise(kd3[:].rearrange("p d t -> p (d t)"), P, "kd3")
+        acc3 = ps.tile([P, P], F32, name="acc3")
+        product(acc3[:], main_mx, slice(0, Q), kd3_mx, slice(0, P), True, True)
+        finish(acc[:], 0, 3 * P, "y012")
+        finish(acc3[:], 3 * P, P, "y3")

@@ -70,18 +70,24 @@ def tile_attend_gpairrank_kernel(tc, query, cand_words, cand_scales, crow, psz, 
             )
 
         def turned_difference(j, sb_tag, ps_tag):
+            dealt = j in (3,)
             pair = sb.tile([P, 2, I], F32, name="pair%d" % j, tag=sb_tag, align_bytes=64)
             nc.vector.tensor_scalar(pair[:, 0, :], row_win[j][:].indirect(list_a[:]), -1.0, 0.0, ALU.mult, ALU.add)
-            nc.vector.tensor_copy(
-                pair[:, 1, :].bitcast(U32).rearrange("p (t s) -> p s t", t=PACK),
-                row_win[j][:, 0:T].bitcast(U32).indirect(list_b[:]),
-            )
+            if dealt:
+                nc.vector.tensor_copy(
+                    pair[:, 1, :].bitcast(U32).rearrange("p (t s) -> p s t", t=PACK),
+                    row_win[j][:, 0:T].bitcast(U32).indirect(list_b[:]),
+                )
+                kb = [pair[:, 1, t * P : (t + 1) * P] for t in range(PACK)]
+            else:
+                nc.vector.tensor_copy(pair[:, 1, :], row_win[j][:, 0:T].indirect(list_b[:]))
+                kb = [pair[:, 1, t:I:PACK] for t in range(PACK)]
             bank = ps.tile([P, PACK, P], F32, name="kd_bank%d" % j, tag=ps_tag)
             for t in range(PACK):
                 nc.tensor.matmul(bank[:, t, :], pair[:, 0, t:I:PACK], ident[:], start=(t == 0), stop=False, is_transpose=True)
             for t in range(PACK):
                 nc.tensor.matmul(
-                    bank[:, t, :], pair[:, 1, t * P : (t + 1) * P], ident[:], start=False, stop=(t == PACK - 1), is_transpose=True
+                    bank[:, t, :], kb[t], ident[:], start=False, stop=(t == PACK - 1), is_transpose=True
                 )
             return bank
 
@@ -126,7 +132,17 @@ def tile_attend_gpairrank_kernel(tc, query, cand_words, cand_scales, crow, psz, 
         product(z[:], q_mx, slice(0, Q), (word_a, scale_a), slice(0, I), True, False)
         product(z[:], q_mx, slice(Q, 2 * Q), (word_b, scale_b), slice(0, I), False, True)
 
-        grouped = sb.tile([P, TILES, P, PACK], BF16, name="grouped", tag="grouped", align_bytes=64)
+        codes = sb.tile([P, Q + D], U32, name="codes", align_bytes=64)
+        scales = sb.tile([P, Q + D], U8, name="scales", align_bytes=64)
+        second = (codes, scales)
+
+        def quantise_into(grouped, first, width):
+            cols = slice(first, first + width)
+            nc.vector.quantize_mx(out=codes[:, cols].bitcast(FP8X4), scales=scales[:, cols], in_=grouped)
+
+        st_kd0 = sb.tile([P, 2, P, PACK], BF16, name="st_kd0", align_bytes=64)
+        kd1 = sb.tile([P, P, PACK], BF16, name="kd1", tag="kd_odd", align_bytes=64)
+        kd2 = sb.tile([P, P, PACK], BF16, name="kd2", align_bytes=64)
 
         sig = sb.tile([P, PACK, P], F32, name="sig")
         nc.scalar.activation(sig[:], z[:].rearrange("q (s t) -> q t s", t=PACK), ACT.Sigmoid)
@@ -134,28 +150,30 @@ def tile_attend_gpairrank_kernel(tc, query, cand_words, cand_scales, crow, psz, 
         s_bank = ps.tile([P, PACK, Q], F32, name="s_bank", tag="bank_odd")
         for t in range(PACK):
             nc.tensor.transpose(s_bank[:, t, :], sig[:, t, :], ident[:])
-        scale_and_group(s_bank, psz_t, grouped[:, 0, :, :])
+        scale_and_group(s_bank, psz_t, st_kd0[:, 0, :, :])
         bank1 = turned_difference(1, "pair1", "bank_odd")
-        scale_and_group(bank0, ds1_t, grouped[:, 1, :, :])
+        scale_and_group(bank0, ds1_t, st_kd0[:, 1, :, :])
         bank2 = turned_difference(2, "pair2", "bank_even")
-        scale_and_group(bank1, ds1_t, grouped[:, 2, :, :])
+        scale_and_group(bank1, ds1_t, kd1[:])
         bank3 = turned_difference(3, "pair3", "bank_odd")
-        scale_and_group(bank2, ds1_t, grouped[:, 3, :, :])
+        scale_and_group(bank2, ds1_t, kd2[:])
 
-        main_mx = quantise(grouped[:].rearrange("p j d t -> p (j d t)"), TILES * P, "main")
-        acc = ps.tile([P, 3 * P], F32, name="acc")
-        product(acc[:, 0 : 2 * P], main_mx, slice(0, Q), main_mx, slice(P, 3 * P), True, True)
-        product(acc[:, 2 * P : 3 * P], main_mx, slice(0, Q), main_mx, slice(3 * P, 4 * P), True, True)
+        quantise_into(st_kd0[:].rearrange("p j d t -> p (j d t)"), 0, 2 * P)
+        quantise_into(kd1[:].rearrange("p d t -> p (d t)"), 2 * P, P)
+        acc01 = ps.tile([P, 2 * P], F32, name="acc01")
+        product(acc01[:], second, slice(0, Q), second, slice(P, 3 * P), True, True)
 
-        kd3 = sb.tile([P, P, PACK], BF16, name="kd3", tag="grouped", align_bytes=64)
+        kd3 = sb.tile([P, P, PACK], BF16, name="kd3", tag="kd_odd", align_bytes=64)
         nc.vector.tensor_tensor(
             kd3[:],
             bank3[:].rearrange("p t d -> p d t"),
             ds1_t[:].unsqueeze(1).to_broadcast([P, P, PACK]),
             ALU.mult,
         )
-        kd3_mx = quantise(kd3[:].rearrange("p d t -> p (d t)"), P, "kd3")
-        acc3 = ps.tile([P, P], F32, name="acc3")
-        product(acc3[:], main_mx, slice(0, Q), kd3_mx, slice(0, P), True, True)
-        finish(acc[:], 0, 3 * P, "y012")
-        finish(acc3[:], 3 * P, P, "y3")
+        acc23 = ps.tile([P, 2 * P], F32, name="acc23")
+        quantise_into(kd2[:].rearrange("p d t -> p (d t)"), 3 * P, P)
+        product(acc23[:, 0:P], second, slice(0, Q), second, slice(3 * P, 4 * P), True, True)
+        quantise_into(kd3[:].rearrange("p d t -> p (d t)"), 4 * P, P)
+        product(acc23[:, P : 2 * P], second, slice(0, Q), second, slice(4 * P, 5 * P), True, True)
+        finish(acc01[:], 0, 2 * P, "y01")
+        finish(acc23[:], 2 * P, 2 * P, "y23")

@@ -48,11 +48,11 @@ def tile_attend_gpairrank_kernel(tc, query, cand_words, cand_scales, crow, psz, 
                 in_=cand_scales[0, 4 * quad : 4 * quad + 4, :].bitcast(I32),
             )
         nc.sync.dma_start(list_b[:], offs2)
-        nc.sync.dma_start(out=psz_t[:], in_=psz.rearrange("o (p t) -> (o p) t", t=PACK))
+        nc.sync.dma_start(out=q_raw[:], in_=query.rearrange("(p t) q -> p t q", t=PACK))
         nc.vector.memset(warm[:], 0.0)
         nc.scalar.activation(warm_out[:], warm[:], ACT.Sigmoid)
         nc.sync.dma_start(out=word_win[:], in_=cand_words[0].rearrange("p n t -> p (n t)").bitcast(I32))
-        nc.sync.dma_start(out=q_raw[:], in_=query.rearrange("(p t) q -> p t q", t=PACK))
+        nc.sync.dma_start(out=psz_t[:], in_=psz.rearrange("o (p t) -> (o p) t", t=PACK))
         nc.sync.dma_start(out=row_win[0][:, 0:T], in_=crow[0:P, :])
         nc.sync.dma_start(out=ds1_t[:], in_=ds1.rearrange("(p t) o -> p (t o)", t=PACK))
         for j in range(1, TILES):
@@ -70,9 +70,18 @@ def tile_attend_gpairrank_kernel(tc, query, cand_words, cand_scales, crow, psz, 
             )
 
         def turned_difference(j, sb_tag, ps_tag):
-            dealt = j in (3,)
+            dealt = j in (2, 3)
             pair = sb.tile([P, 2, I], F32, name="pair%d" % j, tag=sb_tag, align_bytes=64)
-            nc.vector.tensor_scalar(pair[:, 0, :], row_win[j][:].indirect(list_a[:]), -1.0, 0.0, ALU.mult, ALU.add)
+            if j in (0,):
+                nc.vector.tensor_copy(pair[:, 0, :], row_win[j][:, 0:T].indirect(list_a[:]))
+                neg = sb.tile([P, PACK, P], F32, name="neg%d" % j)
+                nc.scalar.activation(
+                    neg[:].rearrange("p t s -> p s t"), pair[:, 0, :].rearrange("p (s t) -> p s t", t=PACK), ACT.Copy, scale=-1.0
+                )
+                ka = [neg[:, t, :] for t in range(PACK)]
+            else:
+                nc.vector.tensor_scalar(pair[:, 0, :], row_win[j][:].indirect(list_a[:]), -1.0, 0.0, ALU.mult, ALU.add)
+                ka = [pair[:, 0, t:I:PACK] for t in range(PACK)]
             if dealt:
                 nc.vector.tensor_copy(
                     pair[:, 1, :].bitcast(U32).rearrange("p (t s) -> p s t", t=PACK),
@@ -84,7 +93,7 @@ def tile_attend_gpairrank_kernel(tc, query, cand_words, cand_scales, crow, psz, 
                 kb = [pair[:, 1, t:I:PACK] for t in range(PACK)]
             bank = ps.tile([P, PACK, P], F32, name="kd_bank%d" % j, tag=ps_tag)
             for t in range(PACK):
-                nc.tensor.matmul(bank[:, t, :], pair[:, 0, t:I:PACK], ident[:], start=(t == 0), stop=False, is_transpose=True)
+                nc.tensor.matmul(bank[:, t, :], ka[t], ident[:], start=(t == 0), stop=False, is_transpose=True)
             for t in range(PACK):
                 nc.tensor.matmul(
                     bank[:, t, :], kb[t], ident[:], start=False, stop=(t == PACK - 1), is_transpose=True
@@ -170,10 +179,12 @@ def tile_attend_gpairrank_kernel(tc, query, cand_words, cand_scales, crow, psz, 
             ds1_t[:].unsqueeze(1).to_broadcast([P, P, PACK]),
             ALU.mult,
         )
-        acc23 = ps.tile([P, 2 * P], F32, name="acc23")
+        acc2 = ps.tile([P, P], F32, name="acc2")
+        acc3 = ps.tile([P, P], F32, name="acc3")
         quantise_into(kd2[:].rearrange("p d t -> p (d t)"), 3 * P, P)
-        product(acc23[:, 0:P], second, slice(0, Q), second, slice(3 * P, 4 * P), True, True)
+        product(acc2[:], second, slice(0, Q), second, slice(3 * P, 4 * P), True, True)
         quantise_into(kd3[:].rearrange("p d t -> p (d t)"), 4 * P, P)
-        product(acc23[:, P : 2 * P], second, slice(0, Q), second, slice(4 * P, 5 * P), True, True)
+        product(acc3[:], second, slice(0, Q), second, slice(4 * P, 5 * P), True, True)
         finish(acc01[:], 0, 2 * P, "y01")
-        finish(acc23[:], 2 * P, 2 * P, "y23")
+        finish(acc2[:], 2 * P, P, "y2")
+        finish(acc3[:], 3 * P, P, "y3")

@@ -48,11 +48,11 @@ def tile_attend_gpairrank_kernel(tc, query, cand_words, cand_scales, crow, psz, 
                 in_=cand_scales[0, 4 * quad : 4 * quad + 4, :].bitcast(I32),
             )
         nc.sync.dma_start(list_b[:], offs2)
-        nc.sync.dma_start(out=q_raw[:], in_=query.rearrange("(p t) q -> p t q", t=PACK))
+        nc.sync.dma_start(out=psz_t[:], in_=psz.rearrange("o (p t) -> (o p) t", t=PACK))
         nc.vector.memset(warm[:], 0.0)
         nc.scalar.activation(warm_out[:], warm[:], ACT.Sigmoid)
         nc.sync.dma_start(out=word_win[:], in_=cand_words[0].rearrange("p n t -> p (n t)").bitcast(I32))
-        nc.sync.dma_start(out=psz_t[:], in_=psz.rearrange("o (p t) -> (o p) t", t=PACK))
+        nc.sync.dma_start(out=q_raw[:], in_=query.rearrange("(p t) q -> p t q", t=PACK))
         nc.sync.dma_start(out=row_win[0][:, 0:T], in_=crow[0:P, :])
         nc.sync.dma_start(out=ds1_t[:], in_=ds1.rearrange("(p t) o -> p (t o)", t=PACK))
         for j in range(1, TILES):
@@ -60,8 +60,8 @@ def tile_attend_gpairrank_kernel(tc, query, cand_words, cand_scales, crow, psz, 
         nc.sync.dma_start(out=res_t[:], in_=res)
         make_identity(nc, ident[:])
 
-        def scale_and_group(bank, factor, grouped):
-            planes = sb.tile([P, PACK, P], BF16, name="planes")
+        def scale_and_group(bank, factor, grouped, tag):
+            planes = sb.tile([P, PACK, P], BF16, name="planes", tag=tag)
             for t in range(PACK):
                 nc.scalar.activation(planes[:, t, :], bank[:, t, :], ACT.Copy, scale=factor[:, t : t + 1])
             nc.scalar.copy(
@@ -70,18 +70,9 @@ def tile_attend_gpairrank_kernel(tc, query, cand_words, cand_scales, crow, psz, 
             )
 
         def turned_difference(j, sb_tag, ps_tag):
-            dealt = j in (2, 3)
+            dealt = j in (0, 1, 2, 3)
             pair = sb.tile([P, 2, I], F32, name="pair%d" % j, tag=sb_tag, align_bytes=64)
-            if j in (0,):
-                nc.vector.tensor_copy(pair[:, 0, :], row_win[j][:, 0:T].indirect(list_a[:]))
-                neg = sb.tile([P, PACK, P], F32, name="neg%d" % j)
-                nc.scalar.activation(
-                    neg[:].rearrange("p t s -> p s t"), pair[:, 0, :].rearrange("p (s t) -> p s t", t=PACK), ACT.Copy, scale=-1.0
-                )
-                ka = [neg[:, t, :] for t in range(PACK)]
-            else:
-                nc.vector.tensor_scalar(pair[:, 0, :], row_win[j][:].indirect(list_a[:]), -1.0, 0.0, ALU.mult, ALU.add)
-                ka = [pair[:, 0, t:I:PACK] for t in range(PACK)]
+            nc.vector.tensor_scalar(pair[:, 0, :], row_win[j][:].indirect(list_a[:]), -1.0, 0.0, ALU.mult, ALU.add)
             if dealt:
                 nc.vector.tensor_copy(
                     pair[:, 1, :].bitcast(U32).rearrange("p (t s) -> p s t", t=PACK),
@@ -93,7 +84,7 @@ def tile_attend_gpairrank_kernel(tc, query, cand_words, cand_scales, crow, psz, 
                 kb = [pair[:, 1, t:I:PACK] for t in range(PACK)]
             bank = ps.tile([P, PACK, P], F32, name="kd_bank%d" % j, tag=ps_tag)
             for t in range(PACK):
-                nc.tensor.matmul(bank[:, t, :], ka[t], ident[:], start=(t == 0), stop=False, is_transpose=True)
+                nc.tensor.matmul(bank[:, t, :], pair[:, 0, t:I:PACK], ident[:], start=(t == 0), stop=False, is_transpose=True)
             for t in range(PACK):
                 nc.tensor.matmul(
                     bank[:, t, :], kb[t], ident[:], start=False, stop=(t == PACK - 1), is_transpose=True
@@ -150,41 +141,42 @@ def tile_attend_gpairrank_kernel(tc, query, cand_words, cand_scales, crow, psz, 
             nc.vector.quantize_mx(out=codes[:, cols].bitcast(FP8X4), scales=scales[:, cols], in_=grouped)
 
         st_kd0 = sb.tile([P, 2, P, PACK], BF16, name="st_kd0", align_bytes=64)
-        kd1 = sb.tile([P, P, PACK], BF16, name="kd1", tag="kd_odd", align_bytes=64)
-        kd2 = sb.tile([P, P, PACK], BF16, name="kd2", align_bytes=64)
+        kd12 = sb.tile([P, 2, P, PACK], BF16, name="kd12", tag="kd_late", align_bytes=64)
+
+        def scale_on_vector(bank, grouped):
+            nc.vector.tensor_tensor(
+                grouped,
+                bank[:].rearrange("p t d -> p d t"),
+                ds1_t[:].unsqueeze(1).to_broadcast([P, P, PACK]),
+                ALU.mult,
+            )
 
         sig = sb.tile([P, PACK, P], F32, name="sig")
         nc.scalar.activation(sig[:], z[:].rearrange("q (s t) -> q t s", t=PACK), ACT.Sigmoid)
-        bank0 = turned_difference(0, "q_then_pair0", "bank_even")
-        s_bank = ps.tile([P, PACK, Q], F32, name="s_bank", tag="bank_odd")
+        bank0 = turned_difference(0, "q_then_pair0", "bank0")
+        s_bank = ps.tile([P, PACK, Q], F32, name="s_bank", tag="bank_s")
         for t in range(PACK):
             nc.tensor.transpose(s_bank[:, t, :], sig[:, t, :], ident[:])
-        scale_and_group(s_bank, psz_t, st_kd0[:, 0, :, :])
-        bank1 = turned_difference(1, "pair1", "bank_odd")
-        scale_and_group(bank0, ds1_t, st_kd0[:, 1, :, :])
-        bank2 = turned_difference(2, "pair2", "bank_even")
-        scale_and_group(bank1, ds1_t, kd1[:])
-        bank3 = turned_difference(3, "pair3", "bank_odd")
-        scale_and_group(bank2, ds1_t, kd2[:])
+        scale_and_group(bank0, ds1_t, st_kd0[:, 1, :, :], "planes_x")
+        scale_and_group(s_bank, psz_t, st_kd0[:, 0, :, :], "planes_y")
+        bank1 = turned_difference(1, "pair1", "bank1")
+        scale_and_group(bank1, ds1_t, kd12[:, 0, :, :], "planes_x")
+        bank2 = turned_difference(2, "pair2", "bank0")
+        bank3 = turned_difference(3, "pair3", "bank_s")
+        scale_on_vector(bank2, kd12[:, 1, :, :])
 
         quantise_into(st_kd0[:].rearrange("p j d t -> p (j d t)"), 0, 2 * P)
-        quantise_into(kd1[:].rearrange("p d t -> p (d t)"), 2 * P, P)
-        acc01 = ps.tile([P, 2 * P], F32, name="acc01")
-        product(acc01[:], second, slice(0, Q), second, slice(P, 3 * P), True, True)
+        acc0 = ps.tile([P, P], F32, name="acc0")
+        product(acc0[:], second, slice(0, Q), second, slice(P, 2 * P), True, True)
+        quantise_into(kd12[:].rearrange("p j d t -> p (j d t)"), 2 * P, 2 * P)
+        acc12 = ps.tile([P, 2 * P], F32, name="acc12")
+        product(acc12[:], second, slice(0, Q), second, slice(2 * P, 4 * P), True, True)
 
-        kd3 = sb.tile([P, P, PACK], BF16, name="kd3", tag="kd_odd", align_bytes=64)
-        nc.vector.tensor_tensor(
-            kd3[:],
-            bank3[:].rearrange("p t d -> p d t"),
-            ds1_t[:].unsqueeze(1).to_broadcast([P, P, PACK]),
-            ALU.mult,
-        )
-        acc2 = ps.tile([P, P], F32, name="acc2")
-        acc3 = ps.tile([P, P], F32, name="acc3")
-        quantise_into(kd2[:].rearrange("p d t -> p (d t)"), 3 * P, P)
-        product(acc2[:], second, slice(0, Q), second, slice(3 * P, 4 * P), True, True)
+        kd3 = sb.tile([P, P, PACK], BF16, name="kd3", tag="kd_late", align_bytes=64)
+        scale_on_vector(bank3, kd3[:])
+        finish(acc12[:], P, 2 * P, "y12")
         quantise_into(kd3[:].rearrange("p d t -> p (d t)"), 4 * P, P)
+        acc3 = ps.tile([P, P], F32, name="acc3")
         product(acc3[:], second, slice(0, Q), second, slice(4 * P, 5 * P), True, True)
-        finish(acc01[:], 0, 2 * P, "y01")
-        finish(acc2[:], 2 * P, P, "y2")
+        finish(acc0[:], 0, P, "y0")
         finish(acc3[:], 3 * P, P, "y3")

from contextlib import ExitStack

import concourse.mybir as mybir
from concourse.masks import make_identity

D, T, I, Q = 512, 1024, 512, 128
P = 128
PACK = 4
TILES = D // P
FLOPS = 2 * Q * I * D * 3

F32 = mybir.dt.float32
BF16 = mybir.dt.bfloat16
I32 = mybir.dt.int32
U32 = mybir.dt.uint32
U16 = mybir.dt.uint16
U8 = mybir.dt.uint8
FP8X4 = mybir.dt.float8_e4m3fn_x4
ACT = mybir.ActivationFunctionType
ALU = mybir.AluOpType


def tile_attend_gpairrank_kernel(tc, query, cand_words, cand_scales, crow, psz, ds1, res, offs, offs2, out):
    nc = tc.nc
    with ExitStack() as ctx:
        sb = ctx.enter_context(tc.tile_pool(name="sb", bufs=1))
        ps = ctx.enter_context(tc.psum_pool(name="ps", bufs=1))

        list_a = sb.tile([P, I // 16], U16, name="list_a")
        list_b = sb.tile([P, I // 16], U16, name="list_b")
        scale_win = sb.tile([P, T], U8, name="scale_win")
        word_win = sb.tile([P, T], I32, name="word_win")
        q_raw = sb.tile([P, PACK, Q], F32, name="q_raw")
        row_win = [sb.tile([P, 2 * T], F32, name="row_win%d" % j) for j in range(TILES)]
        psz_t = sb.tile([P, PACK], F32, name="psz_t")
        ds1_t = sb.tile([P, PACK], F32, name="ds1_t")
        res_t = sb.tile([P, D], F32, name="res_t")
        ident = sb.tile([P, P], F32, name="ident")
        warm = sb.tile([P, 8], F32, name="warm")
        warm_out = sb.tile([P, 8], F32, name="warm_out")

        nc.gpsimd.memset(scale_win[:].bitcast(I32), 0)
        nc.sync.dma_start(list_a[:], offs)
        for quad in range(4):
            queue = nc.sync if quad < 2 else nc.scalar
            queue.dma_start(
                out=scale_win[32 * quad : 32 * quad + 4, :].bitcast(I32),
                in_=cand_scales[0, 4 * quad : 4 * quad + 4, :].bitcast(I32),
            )
        nc.sync.dma_start(list_b[:], offs2)
        nc.sync.dma_start(out=psz_t[:], in_=psz.rearrange("o (p t) -> (o p) t", t=PACK))
        nc.vector.memset(warm[:], 0.0)
        nc.scalar.activation(warm_out[:], warm[:], ACT.Sigmoid)
        nc.sync.dma_start(out=word_win[:], in_=cand_words[0].rearrange("p n t -> p (n t)").bitcast(I32))
        nc.sync.dma_start(out=q_raw[:], in_=query.rearrange("(p t) q -> p t q", t=PACK))
        nc.sync.dma_start(out=row_win[0][:, 0:T], in_=crow[0:P, :])
        nc.sync.dma_start(out=ds1_t[:], in_=ds1.rearrange("(p t) o -> p (t o)", t=PACK))
        for j in range(1, TILES):
            nc.sync.dma_start(out=row_win[j][:, 0:T], in_=crow[j * P : (j + 1) * P, :])
        nc.sync.dma_start(out=res_t[:], in_=res)
        make_identity(nc, ident[:])

        def scale_and_group(bank, factor, grouped, tag):
            planes = sb.tile([P, PACK, P], BF16, name="planes", tag=tag)
            for t in range(PACK):
                nc.scalar.activation(planes[:, t, :], bank[:, t, :], ACT.Copy, scale=factor[:, t : t + 1])
            nc.scalar.copy(
                out=grouped.rearrange("p (c i) t -> p c t i", i=4),
                in_=planes[:].rearrange("p t (c i) -> p c t i", i=4),
            )

        def turned_difference(j, sb_tag, ps_tag):
            dealt = j in (0, 1, 2, 3)
            pair = sb.tile([P, 2, I], F32, name="pair%d" % j, tag=sb_tag, align_bytes=64)
            nc.vector.tensor_scalar(pair[:, 0, :], row_win[j][:].indirect(list_a[:]), -1.0, 0.0, ALU.mult, ALU.add)
            if dealt:
                nc.vector.tensor_copy(
                    pair[:, 1, :].bitcast(U32).rearrange("p (t s) -> p s t", t=PACK),
                    row_win[j][:, 0:T].bitcast(U32).indirect(list_b[:]),
                )
                kb = [pair[:, 1, t * P : (t + 1) * P] for t in range(PACK)]
            else:
                nc.vector.tensor_copy(pair[:, 1, :], row_win[j][:, 0:T].indirect(list_b[:]))
                kb = [pair[:, 1, t:I:PACK] for t in range(PACK)]
            bank = ps.tile([P, PACK, P], F32, name="kd_bank%d" % j, tag=ps_tag)
            for t in range(PACK):
                nc.tensor.matmul(bank[:, t, :], pair[:, 0, t:I:PACK], ident[:], start=(t == 0), stop=False, is_transpose=True)
            for t in range(PACK):
                nc.tensor.matmul(
                    bank[:, t, :], kb[t], ident[:], start=False, stop=(t == PACK - 1), is_transpose=True
                )
            return bank

        def quantise(grouped, width, name):
            codes = sb.tile([P, width], U32, name=name + "_codes", align_bytes=64)
            scales = sb.tile([P, width], U8, name=name + "_scales", align_bytes=64)
            nc.vector.quantize_mx(out=codes[:].bitcast(FP8X4), scales=scales[:], in_=grouped)
            return codes, scales

        def product(acc, lhs, lhs_cols, rhs, rhs_cols, start, stop):
            nc.tensor.matmul_mx(
                out=acc,
                lhsT=lhs[0][:, lhs_cols].bitcast(FP8X4),
                lhsT_scale=lhs[1][:, lhs_cols],
                rhs=rhs[0][:, rhs_cols].bitcast(FP8X4),
                rhs_scale=rhs[1][:, rhs_cols],
                start=start,
                stop=stop,
            )

        def finish(acc, first, width, name):
            cols = slice(first, first + width)
            y = sb.tile([P, width], F32, name=name)
            nc.vector.tensor_tensor(y[:], acc, res_t[:, cols], ALU.add)
            nc.sync.dma_start(out=out[:, cols], in_=y[:])

        scale_a = sb.tile([P, I], U8, name="scale_a", align_bytes=64)
        scale_b = sb.tile([P, I], U8, name="scale_b", align_bytes=64)
        nc.vector.tensor_copy(scale_a[:], scale_win[:].indirect(list_a[:]))
        nc.vector.tensor_copy(scale_b[:], scale_win[:].indirect(list_b[:]))
        word_a = sb.tile([P, I], U32, name="word_a", align_bytes=64)
        word_b = sb.tile([P, I], U32, name="word_b", align_bytes=64)
        nc.vector.tensor_copy(word_a[:], word_win[:].bitcast(U32).indirect(list_a[:]))
        nc.vector.tensor_copy(word_b[:], word_win[:].bitcast(U32).indirect(list_b[:]))

        q_grp = sb.tile([P, 2, Q, PACK], BF16, name="q_grp", tag="q_then_pair0", align_bytes=64)
        for u, sign in enumerate((-1.0, 1.0)):
            nc.scalar.activation(q_grp[:, u, :, :], q_raw[:].rearrange("p t q -> p q t"), ACT.Copy, scale=sign)
        q_mx = quantise(q_grp[:].rearrange("p u q t -> p (u q t)"), 2 * Q, "q")

        z = ps.tile([P, I], F32, name="z")
        product(z[:], q_mx, slice(0, Q), (word_a, scale_a), slice(0, I), True, False)
        product(z[:], q_mx, slice(Q, 2 * Q), (word_b, scale_b), slice(0, I), False, True)

        codes = sb.tile([P, Q + D], U32, name="codes", align_bytes=64)
        scales = sb.tile([P, Q + D], U8, name="scales", align_bytes=64)
        second = (codes, scales)

        def quantise_into(grouped, first, width):
            cols = slice(first, first + width)
            nc.vector.quantize_mx(out=codes[:, cols].bitcast(FP8X4), scales=scales[:, cols], in_=grouped)

        st_kd0 = sb.tile([P, 2, P, PACK], BF16, name="st_kd0", align_bytes=64)
        kd12 = sb.tile([P, 2, P, PACK], BF16, name="kd12", tag="kd_late", align_bytes=64)

        def scale_on_vector(bank, grouped):
            nc.vector.tensor_tensor(
                grouped,
                bank[:].rearrange("p t d -> p d t"),
                ds1_t[:].unsqueeze(1).to_broadcast([P, P, PACK]),
                ALU.mult,
            )

        sig = sb.tile([P, PACK, P], F32, name="sig")
        nc.scalar.activation(sig[:], z[:].rearrange("q (s t) -> q t s", t=PACK), ACT.Sigmoid)
        bank0 = turned_difference(0, "q_then_pair0", "bank0")
        s_bank = ps.tile([P, PACK, Q], F32, name="s_bank", tag="bank_s")
        for t in range(PACK):
            nc.tensor.transpose(s_bank[:, t, :], sig[:, t, :], ident[:])
        scale_and_group(bank0, ds1_t, st_kd0[:, 1, :, :], "planes_x")
        scale_and_group(s_bank, psz_t, st_kd0[:, 0, :, :], "planes_y")
        bank1 = turned_difference(1, "pair1", "bank1")
        scale_and_group(bank1, ds1_t, kd12[:, 0, :, :], "planes_x")
        bank2 = turned_difference(2, "pair2", "bank0")
        bank3 = turned_difference(3, "pair3", "bank_s")
        scale_on_vector(bank2, kd12[:, 1, :, :])

        quantise_into(st_kd0[:].rearrange("p j d t -> p (j d t)"), 0, 2 * P)
        acc0 = ps.tile([P, P], F32, name="acc0")
        product(acc0[:], second, slice(0, Q), second, slice(P, 2 * P), True, True)
        quantise_into(kd12[:].rearrange("p j d t -> p (j d t)"), 2 * P, 2 * P)
        acc12 = ps.tile([P, 2 * P], F32, name="acc12")
        product(acc12[:], second, slice(0, Q), second, slice(2 * P, 4 * P), True, True)

        kd3 = sb.tile([P, P, PACK], BF16, name="kd3", tag="kd_late", align_bytes=64)
        scale_on_vector(bank3, kd3[:])
        finish(acc12[:], P, 2 * P, "y12")
        quantise_into(kd3[:].rearrange("p d t -> p (d t)"), 4 * P, P)
        acc3 = ps.tile([P, P], F32, name="acc3")
        product(acc3[:], second, slice(0, Q), second, slice(4 * P, 5 * P), True, True)
        finish(acc0[:], 0, P, "y0")
        finish(acc3[:], 3 * P, P, "y3")
